import numpy as np
import ml_dtypes


def mxq(x, axis, fmt="e4m3"):
    dtype, down = {"e4m3": (ml_dtypes.float8_e4m3fn, 7), "e5m2": (ml_dtypes.float8_e5m2, 14)}[fmt]
    v = np.moveaxis(np.asarray(x, np.float32).astype(ml_dtypes.bfloat16).astype(np.float64), axis, -1)
    blocks = v.reshape(v.shape[:-1] + (-1, 32))
    amax = np.abs(blocks).max(-1, keepdims=True)
    byte = np.maximum(np.where(amax > 0, np.frexp(amax)[1] - 1 + 127, 0) - down, 1)
    scale = np.exp2(byte - 127.0)
    codes = (blocks / scale).astype(np.float32).astype(dtype).astype(np.float64)
    return np.moveaxis((codes * scale).reshape(v.shape), -1, axis)


WIDE = False


def mx_kscale(k):
    if not WIDE:
        return np.ones(k)
    levels = np.array([10, -10, 5, -5, 0])
    if k % 512:
        return np.exp2(np.random.permutation(np.resize(levels, k // 32))).repeat(32)
    a = np.empty((k // 512, 16))
    for p in range(k // 512):
        a[p, :8] = np.random.permutation(np.resize(levels, 8))
        for g in range(8):
            far = levels[np.abs(levels - a[p, g]) >= 10]
            a[p, g + 8] = far[np.random.randint(len(far))]
    return np.exp2(a.ravel()).repeat(32)


def f64(x):
    return np.asarray(x).astype(np.float64)


def striped(idx):
    return np.tile(idx.reshape(-1, 16).T, (8, 1)).astype(np.uint16)


def unstriped(offs):
    return offs[:16].T.reshape(-1).astype(np.int64)


K, T, D, S, V, N = 1024, 2048, 8, 4096, 512, 128


def setup_inputs():
    n = np.random.standard_normal
    s = mx_kscale(K)[:, None]
    return {
        "xT": (n((K, T)) * s).astype(np.float32),
        "w": (n((K, N)) / np.sqrt(K) / s).astype(np.float32),
        "b": (0.3 * n((N, 1))).astype(np.float32),
        "offs": striped(np.concatenate([np.random.permutation(T)[:V] for _ in range(D)])),
    }


def reference(xT, w, b, offs):
    idx = unstriped(offs)
    x = np.empty((K, V))
    for l in range(D):
        r = l // 4 * (4 * K // D) + l % 4 + 4 * np.arange(K // D)
        x[r] = f64(xT)[r][:, idx[l * V:(l + 1) * V]]
    xq = mxq(x, 0, "e4m3")
    return (mxq(f64(w), 0, "e4m3").T @ xq) + f64(b)

@@ -1,0 +1,103 @@
+from contextlib import ExitStack
+
+import concourse.mybir as mybir
+
+K, T, LEVELS, V, N = 1024, 2048, 8, 512, 128
+FLOPS = 2 * K * N * V
+
+F32 = mybir.dt.float32
+BF16 = mybir.dt.bfloat16
+U32 = mybir.dt.uint32
+U16 = mybir.dt.uint16
+U8 = mybir.dt.uint8
+FP8X4 = mybir.dt.float8_e4m3fn_x4
+ADD = mybir.AluOpType.add
+IDENTITY = mybir.ActivationFunctionType.Identity
+
+P = 128
+PACK = 4
+PASSES = K // (P * PACK)
+HALF = V // 2
+COLS = V // 16
+
+
+def tile_picked_grid_lin_bias_sub_l_kernel(tc, xT, w, b, offs, out):
+    nc = tc.nc
+    x_rows = xT.rearrange("(g p t) c -> g t p c", p=P, t=PACK)
+    w_rows = w.rearrange("(g p t) m -> g p t m", p=P, t=PACK)
+
+    with ExitStack() as ctx:
+        keep = ctx.enter_context(tc.tile_pool(name="keep", bufs=1))
+        psum = ctx.enter_context(tc.psum_pool(name="psum", bufs=1))
+
+        offsets = keep.tile([P, LEVELS * COLS], U16, name="offsets")
+        bias = keep.tile([P, 1], F32, name="bias")
+        tables = [keep.tile([P, T], F32, name=f"table{l}") for l in range(LEVELS)]
+        w_raw = [keep.tile([P, PACK, N], F32, name=f"w_raw{g}") for g in range(PASSES)]
+        w_grouped = [keep.tile([P, N, PACK], BF16, name=f"w_grouped{g}", align_bytes=64) for g in range(PASSES)]
+        w_codes = [keep.tile([P, N], U32, name=f"w_codes{g}", align_bytes=64) for g in range(PASSES)]
+        w_scales = [keep.tile([P, N], U8, name=f"w_scales{g}", align_bytes=64) for g in range(PASSES)]
+        grouped = [keep.tile([P, V, PACK], BF16, name=f"grouped{g}", align_bytes=64) for g in range(PASSES)]
+        codes = [keep.tile([P, V], U32, name=f"codes{g}", align_bytes=64) for g in range(PASSES)]
+        scales = [keep.tile([P, V], U8, name=f"scales{g}", align_bytes=64) for g in range(PASSES)]
+        acc = [psum.tile([N, HALF], F32, name=f"acc{h}") for h in range(2)]
+        result = [keep.tile([N, HALF], F32, name=f"result{h}") for h in range(2)]
+
+        nc.sync.dma_start(offsets[:], offs)
+        nc.gpsimd.dma_start(bias[:], b)
+        for l in range(LEVELS):
+            nc.sync.dma_start(tables[l][:], x_rows[l // PACK, l % PACK])
+        for g in range(PASSES):
+            nc.sync.dma_start(w_raw[g][:], w_rows[g])
+
+        def gather(l, v0, v1):
+            picked = offsets[:, l * COLS + v0 // 16 : l * COLS + v1 // 16]
+            nc.vector.tensor_copy(grouped[l // PACK][:, v0:v1, l % PACK], tables[l][:].indirect(picked))
+
+        def quantize(g, v0, v1):
+            nc.vector.quantize_mx(
+                out=codes[g][:, v0:v1].bitcast(FP8X4),
+                scales=scales[g][:, v0:v1],
+                in_=grouped[g][:, v0:v1, :].rearrange("p v t -> p (v t)"),
+            )
+
+        def quantize_w(g):
+            nc.vector.quantize_mx(
+                out=w_codes[g][:].bitcast(FP8X4),
+                scales=w_scales[g][:],
+                in_=w_grouped[g][:].rearrange("p m t -> p (m t)"),
+            )
+
+        def multiply(g, h):
+            v0, v1 = h * HALF, (h + 1) * HALF
+            nc.tensor.matmul_mx(
+                out=acc[h][:],
+                lhsT=w_codes[g][:].bitcast(FP8X4),
+                lhsT_scale=w_scales[g][:],
+                rhs=codes[g][:, v0:v1].bitcast(FP8X4),
+                rhs_scale=scales[g][:, v0:v1],
+                start=(g == 0),
+                stop=(g == PASSES - 1),
+            )
+
+        for l in range(PACK):
+            gather(l, 0, V)
+        gather(4, 0, V)
+        quantize(0, 0, V)
+        gather(5, 0, V)
+        gather(6, 0, V)
+        gather(7, 0, HALF)
+        gather(7, HALF, V)
+        for g in range(PASSES):
+            nc.scalar.copy(w_grouped[g][:], w_raw[g][:].rearrange("p t m -> p m t"))
+        quantize(1, 0, HALF)
+        quantize_w(0)
+        quantize_w(1)
+        quantize(1, HALF, V)
+        for h in range(2):
+            multiply(0, h)
+            multiply(1, h)
+        nc.vector.tensor_scalar(result[0][:], acc[0][:], bias[:], None, ADD)
+        nc.sync.dma_start(out[:, 0:HALF], result[0][:])
+        nc.scalar.activation(result[1][:], acc[1][:], IDENTITY, bias=bias[:])
+        nc.scalar.dma_start(out[:, HALF:V], result[1][:])

@@ -44,7 +44,7 @@ def tile_picked_grid_lin_bias_sub_l_kernel(tc, xT, w, b, offs, out):
         result = [keep.tile([N, HALF], F32, name=f"result{h}") for h in range(2)]
 
         nc.sync.dma_start(offsets[:], offs)
-        nc.gpsimd.dma_start(bias[:], b)
+        nc.scalar.dma_start(bias[:], b)
         for l in range(LEVELS):
             nc.sync.dma_start(tables[l][:], x_rows[l // PACK, l % PACK])
         for g in range(PASSES):
@@ -90,13 +90,13 @@ def tile_picked_grid_lin_bias_sub_l_kernel(tc, xT, w, b, offs, out):
         gather(7, HALF, V)
         for g in range(PASSES):
             nc.scalar.copy(w_grouped[g][:], w_raw[g][:].rearrange("p t m -> p m t"))
-        quantize(1, 0, HALF)
         quantize_w(0)
+        quantize(1, 0, HALF)
         quantize_w(1)
         quantize(1, HALF, V)
-        for h in range(2):
-            multiply(0, h)
-            multiply(1, h)
+        for g in range(PASSES):
+            for h in range(2):
+                multiply(g, h)
         nc.vector.tensor_scalar(result[0][:], acc[0][:], bias[:], None, ADD)
         nc.sync.dma_start(out[:, 0:HALF], result[0][:])
         nc.scalar.activation(result[1][:], acc[1][:], IDENTITY, bias=bias[:])

@@ -18,6 +18,7 @@ P = 128
 PACK = 4
 PASSES = K // (P * PACK)
 HALF = V // 2
+CHUNKS = ((0, 256), (256, 384), (384, 512))
 COLS = V // 16
 
 
@@ -40,15 +41,15 @@ def tile_picked_grid_lin_bias_sub_l_kernel(tc, xT, w, b, offs, out):
         grouped = [keep.tile([P, V, PACK], BF16, name=f"grouped{g}", align_bytes=64) for g in range(PASSES)]
         codes = [keep.tile([P, V], U32, name=f"codes{g}", align_bytes=64) for g in range(PASSES)]
         scales = [keep.tile([P, V], U8, name=f"scales{g}", align_bytes=64) for g in range(PASSES)]
-        acc = [psum.tile([N, HALF], F32, name=f"acc{h}") for h in range(2)]
-        result = [keep.tile([N, HALF], F32, name=f"result{h}") for h in range(2)]
+        acc = [psum.tile([N, v1 - v0], F32, name=f"acc{v0}") for v0, v1 in CHUNKS]
+        result = [keep.tile([N, v1 - v0], F32, name=f"result{v0}") for v0, v1 in CHUNKS]
 
         nc.sync.dma_start(offsets[:], offs)
-        nc.scalar.dma_start(bias[:], b)
         for l in range(LEVELS):
             nc.sync.dma_start(tables[l][:], x_rows[l // PACK, l % PACK])
         for g in range(PASSES):
             nc.sync.dma_start(w_raw[g][:], w_rows[g])
+        nc.sync.dma_start(bias[:], b)
 
         def gather(l, v0, v1):
             picked = offsets[:, l * COLS + v0 // 16 : l * COLS + v1 // 16]
@@ -69,7 +70,7 @@ def tile_picked_grid_lin_bias_sub_l_kernel(tc, xT, w, b, offs, out):
             )
 
         def multiply(g, h):
-            v0, v1 = h * HALF, (h + 1) * HALF
+            v0, v1 = CHUNKS[h]
             nc.tensor.matmul_mx(
                 out=acc[h][:],
                 lhsT=w_codes[g][:].bitcast(FP8X4),
@@ -91,13 +92,16 @@ def tile_picked_grid_lin_bias_sub_l_kernel(tc, xT, w, b, offs, out):
         for g in range(PASSES):
             nc.scalar.copy(w_grouped[g][:], w_raw[g][:].rearrange("p t m -> p m t"))
         quantize_w(0)
-        quantize(1, 0, HALF)
+        quantize(1, *CHUNKS[0])
         quantize_w(1)
-        quantize(1, HALF, V)
+        quantize(1, *CHUNKS[1])
+        quantize(1, *CHUNKS[2])
         for g in range(PASSES):
-            for h in range(2):
+            for h in range(len(CHUNKS)):
                 multiply(g, h)
-        nc.vector.tensor_scalar(result[0][:], acc[0][:], bias[:], None, ADD)
-        nc.sync.dma_start(out[:, 0:HALF], result[0][:])
-        nc.scalar.activation(result[1][:], acc[1][:], IDENTITY, bias=bias[:])
-        nc.scalar.dma_start(out[:, HALF:V], result[1][:])
+        for h, (v0, v1) in enumerate(CHUNKS):
+            if h == len(CHUNKS) - 1:
+                nc.vector.tensor_scalar(result[h][:], acc[h][:], bias[:], None, ADD)
+            else:
+                nc.scalar.activation(result[h][:], acc[h][:], IDENTITY, bias=bias[:])
+            nc.sync.dma_start(out[:, v0:v1], result[h][:])

from contextlib import ExitStack

import concourse.mybir as mybir

K, T, LEVELS, V, N = 1024, 2048, 8, 512, 128
FLOPS = 2 * K * N * V

F32 = mybir.dt.float32
BF16 = mybir.dt.bfloat16
U32 = mybir.dt.uint32
U16 = mybir.dt.uint16
U8 = mybir.dt.uint8
FP8X4 = mybir.dt.float8_e4m3fn_x4
ADD = mybir.AluOpType.add
IDENTITY = mybir.ActivationFunctionType.Identity

P = 128
PACK = 4
PASSES = K // (P * PACK)
HALF = V // 2
CHUNKS = ((0, 256), (256, 384), (384, 512))
COLS = V // 16


def tile_picked_grid_lin_bias_sub_l_kernel(tc, xT, w, b, offs, out):
    nc = tc.nc
    x_rows = xT.rearrange("(g p t) c -> g t p c", p=P, t=PACK)
    w_rows = w.rearrange("(g p t) m -> g p t m", p=P, t=PACK)

    with ExitStack() as ctx:
        keep = ctx.enter_context(tc.tile_pool(name="keep", bufs=1))
        psum = ctx.enter_context(tc.psum_pool(name="psum", bufs=1))

        offsets = keep.tile([P, LEVELS * COLS], U16, name="offsets")
        bias = keep.tile([P, 1], F32, name="bias")
        tables = [keep.tile([P, T], F32, name=f"table{l}") for l in range(LEVELS)]
        w_raw = [keep.tile([P, PACK, N], F32, name=f"w_raw{g}") for g in range(PASSES)]
        w_grouped = [keep.tile([P, N, PACK], BF16, name=f"w_grouped{g}", align_bytes=64) for g in range(PASSES)]
        w_codes = [keep.tile([P, N], U32, name=f"w_codes{g}", align_bytes=64) for g in range(PASSES)]
        w_scales = [keep.tile([P, N], U8, name=f"w_scales{g}", align_bytes=64) for g in range(PASSES)]
        grouped = [keep.tile([P, V, PACK], BF16, name=f"grouped{g}", align_bytes=64) for g in range(PASSES)]
        codes = [keep.tile([P, V], U32, name=f"codes{g}", align_bytes=64) for g in range(PASSES)]
        scales = [keep.tile([P, V], U8, name=f"scales{g}", align_bytes=64) for g in range(PASSES)]
        acc = [psum.tile([N, v1 - v0], F32, name=f"acc{v0}") for v0, v1 in CHUNKS]
        result = [keep.tile([N, v1 - v0], F32, name=f"result{v0}") for v0, v1 in CHUNKS]

        nc.sync.dma_start(offsets[:], offs)
        for l in range(LEVELS):
            nc.sync.dma_start(tables[l][:], x_rows[l // PACK, l % PACK])
        for g in range(PASSES):
            nc.sync.dma_start(w_raw[g][:], w_rows[g])
        nc.sync.dma_start(bias[:], b)

        def gather(l, v0, v1):
            picked = offsets[:, l * COLS + v0 // 16 : l * COLS + v1 // 16]
            nc.vector.tensor_copy(grouped[l // PACK][:, v0:v1, l % PACK], tables[l][:].indirect(picked))

        def quantize(g, v0, v1):
            nc.vector.quantize_mx(
                out=codes[g][:, v0:v1].bitcast(FP8X4),
                scales=scales[g][:, v0:v1],
                in_=grouped[g][:, v0:v1, :].rearrange("p v t -> p (v t)"),
            )

        def quantize_w(g):
            nc.vector.quantize_mx(
                out=w_codes[g][:].bitcast(FP8X4),
                scales=w_scales[g][:],
                in_=w_grouped[g][:].rearrange("p m t -> p (m t)"),
            )

        def multiply(g, h):
            v0, v1 = CHUNKS[h]
            nc.tensor.matmul_mx(
                out=acc[h][:],
                lhsT=w_codes[g][:].bitcast(FP8X4),
                lhsT_scale=w_scales[g][:],
                rhs=codes[g][:, v0:v1].bitcast(FP8X4),
                rhs_scale=scales[g][:, v0:v1],
                start=(g == 0),
                stop=(g == PASSES - 1),
            )

        for l in range(PACK):
            gather(l, 0, V)
        gather(4, 0, V)
        quantize(0, 0, V)
        gather(5, 0, V)
        gather(6, 0, V)
        gather(7, 0, HALF)
        gather(7, HALF, V)
        for g in range(PASSES):
            nc.scalar.copy(w_grouped[g][:], w_raw[g][:].rearrange("p t m -> p m t"))
        quantize_w(0)
        quantize(1, *CHUNKS[0])
        quantize_w(1)
        quantize(1, *CHUNKS[1])
        quantize(1, *CHUNKS[2])
        for g in range(PASSES):
            for h in range(len(CHUNKS)):
                multiply(g, h)
        for h, (v0, v1) in enumerate(CHUNKS):
            if h == len(CHUNKS) - 1:
                nc.vector.tensor_scalar(result[h][:], acc[h][:], bias[:], None, ADD)
            else:
                nc.scalar.activation(result[h][:], acc[h][:], IDENTITY, bias=bias[:])
            nc.sync.dma_start(out[:, v0:v1], result[h][:])
